import numpy as np
import ml_dtypes


def mxq(x, axis, fmt="e4m3"):
    dtype, down = {"e4m3": (ml_dtypes.float8_e4m3fn, 7), "e5m2": (ml_dtypes.float8_e5m2, 14)}[fmt]
    v = np.moveaxis(np.asarray(x, np.float32).astype(ml_dtypes.bfloat16).astype(np.float64), axis, -1)
    blocks = v.reshape(v.shape[:-1] + (-1, 32))
    amax = np.abs(blocks).max(-1, keepdims=True)
    byte = np.maximum(np.where(amax > 0, np.frexp(amax)[1] - 1 + 127, 0) - down, 1)
    scale = np.exp2(byte - 127.0)
    codes = (blocks / scale).astype(np.float32).astype(dtype).astype(np.float64)
    return np.moveaxis((codes * scale).reshape(v.shape), -1, axis)


WIDE = False


def mx_kscale(k):
    if not WIDE:
        return np.ones(k)
    levels = np.array([10, -10, 5, -5, 0])
    if k % 512:
        return np.exp2(np.random.permutation(np.resize(levels, k // 32))).repeat(32)
    a = np.empty((k // 512, 16))
    for p in range(k // 512):
        a[p, :8] = np.random.permutation(np.resize(levels, 8))
        for g in range(8):
            far = levels[np.abs(levels - a[p, g]) >= 10]
            a[p, g + 8] = far[np.random.randint(len(far))]
    return np.exp2(a.ravel()).repeat(32)


BF16 = ml_dtypes.bfloat16


def bf(x):
    return np.asarray(x, np.float32).astype(BF16)


def f64(x):
    return np.asarray(x).astype(np.float64)


E2M1 = np.array([0.0, 0.5, 1.0, 1.5, 2.0, 3.0, 4.0, 6.0, -0.0, -0.5, -1.0, -1.5, -2.0, -3.0, -4.0, -6.0])


def pack_weight(w, fmt):
    k, n = w.shape
    w = f64(bf(w)).reshape(k // 32, 32, n)
    amax = np.abs(w).max(1)
    if fmt == "e4m3":
        byte = np.frexp(amax)[1] - 1 + 127 - 7
    else:
        mant, ex = np.frexp(amax / 6.0)
        byte = np.where(mant > 0.5, ex, ex - 1) + 127
    byte = np.clip(np.where(amax > 0, byte, 1), 1, 254)
    scaled = (w * np.exp2(127.0 - byte)[:, None, :]).reshape(k, n).astype(np.float32)
    by_word = np.ascontiguousarray(scaled.reshape(k // 512, 128, 4, n).transpose(0, 1, 3, 2))
    if fmt == "e4m3":
        words = by_word.astype(ml_dtypes.float8_e4m3fn).view(np.uint8)
    else:
        c = by_word.astype(ml_dtypes.float4_e2m1fn).view(np.uint8) & 0xF
        words = c[..., 0::2] | (c[..., 1::2] << 4)
    return np.ascontiguousarray(words), np.ascontiguousarray(byte.astype(np.uint8).reshape(k // 512, 16, n))


def unpack_weight(words, scales, fmt):
    g, p, n, _ = words.shape
    if fmt == "e4m3":
        vals = np.ascontiguousarray(words).view(ml_dtypes.float8_e4m3fn).astype(np.float64)
    else:
        nib = np.empty((g, p, n, 4), np.uint8)
        nib[..., 0::2] = words & 0xF
        nib[..., 1::2] = words >> 4
        vals = E2M1[nib]
    vals = vals * np.repeat(np.exp2(scales.astype(np.float64) - 127.0), 8, axis=1)[..., None]
    return vals.transpose(0, 1, 3, 2).reshape(g * 512, n)
def pack4(w):
    words, scales = pack_weight(w, "e2m1")
    return words.reshape(words.shape[0], 128, -1), scales


def unpack4(words, scales):
    return unpack_weight(words.reshape(words.shape[0], 128, -1, 2), scales, "e2m1")


M, K, N = 512, 1024, 3072


def setup_inputs():
    s = mx_kscale(K)
    code = np.random.standard_normal((M, K)) * s
    identity = np.random.standard_normal((K, N)) / np.sqrt(K) / s[:, None]
    expression = np.random.standard_normal((K, N)) / np.sqrt(K) / s[:, None]
    activity = np.random.standard_normal((K, N)) / np.sqrt(K) / s[:, None]
    id_words, id_scales = pack4(identity)
    ex_words, ex_scales = pack_weight(expression, "e4m3")
    return {"code": bf(code),
            "id_words": id_words, "id_scales": id_scales,
            "ex_words": ex_words, "ex_scales": ex_scales,
            "act_basis": bf(activity),
            "mean_shape": bf(np.random.standard_normal(N))}


def reference(code, id_words, id_scales, ex_words, ex_scales, act_basis, mean_shape):
    c = mxq(f64(code), 1, "e4m3")
    ident = c @ unpack4(id_words, id_scales)
    expr = c @ unpack_weight(ex_words, ex_scales, "e4m3")
    act = np.tanh(c @ mxq(f64(act_basis), 0, "e4m3"))
    return f64(mean_shape) + ident + act * expr

@@ -1,0 +1,272 @@
+from contextlib import ExitStack
+
+import concourse.mybir as mybir
+from concourse.masks import make_identity
+
+M, K, N = 512, 1024, 3072
+FLOPS = 3 * 2 * M * K * N
+
+F32 = mybir.dt.float32
+BF16 = mybir.dt.bfloat16
+I32 = mybir.dt.int32
+U32 = mybir.dt.uint32
+U8 = mybir.dt.uint8
+FP8X4 = mybir.dt.float8_e4m3fn_x4
+FP4X4 = mybir.dt.float4_e2m1fn_x4
+ACT = mybir.ActivationFunctionType
+ALU = mybir.AluOpType
+
+P = 128
+G = K // 512
+W = 512
+CHUNKS = N // W
+MT = M // P
+
+
+def tile_morphable_face_decode_s10_kernel(tc, code, id_words, id_scales, ex_words, ex_scales, act_basis, mean_shape, out):
+    nc = tc.nc
+    with ExitStack() as ctx:
+        keep = ctx.enter_context(tc.tile_pool(name="keep", bufs=1))
+        work = ctx.enter_context(tc.tile_pool(name="work", bufs=3))
+        psum = ctx.enter_context(tc.psum_pool(name="psum", bufs=8))
+        ctx.enter_context(tc.manual_schedule())
+
+        one = keep.tile([P, 1], F32, name="one")
+        nc.gpsimd.memset(one[:], 0.0)
+        warm = keep.tile([P, 1], F32, name="warm")
+        nc.scalar.activation(out=warm[:], in_=one[:], func=ACT.Tanh)
+        ident = keep.tile([P, P], F32, name="ident")
+        make_identity(nc, ident[:])
+        idp = keep.tile([P, G, N], U8, name="idp", align_bytes=64)
+        nc.vector.memset(idp[:].rearrange("p g n -> p (g n)").bitcast(I32), 0)
+        exp = keep.tile([P, N], U8, name="exp", align_bytes=64)
+        nc.vector.memset(exp[:].bitcast(I32), 0)
+
+        craw = []
+        for m in range(MT):
+            t = keep.tile([P, K], BF16, name="craw%d" % m, align_bytes=64)
+            nc.sync.dma_start(out=t[:], in_=code[m * P : (m + 1) * P, :])
+            craw.append(t)
+        for q in range(4):
+            nc.sync.dma_start(
+                out=idp[32 * q : 32 * q + 4, :, :].bitcast(I32),
+                in_=id_scales[:, 4 * q : 4 * q + 4, :].rearrange("g r n -> r g n").bitcast(I32),
+            )
+        mean = keep.tile([P, N], BF16, name="mean", align_bytes=64)
+        idw = {}
+        exw = {}
+        raw = {}
+
+        def load_idw(c, width):
+            t = keep.tile([P, G, 2 * width], U8, name="idw%d" % c, align_bytes=64)
+            nc.sync.dma_start(
+                out=t[:].bitcast(I32),
+                in_=id_words[:, :, 2 * W * c : 2 * W * c + 2 * width].rearrange("g p b -> p g b").bitcast(I32),
+            )
+            for i in range(width // W):
+                idw[c + i] = (t, 2 * W * i)
+
+        def load_exw(c):
+            t = keep.tile([P, G, 4 * W], U8, name="exw%d" % c, align_bytes=64)
+            nc.sync.dma_start(
+                out=t[:].bitcast(I32),
+                in_=ex_words.rearrange("g p n t -> p g (n t)")[:, :, 4 * W * c : 4 * W * (c + 1)].bitcast(I32),
+            )
+            exw[c] = t
+
+        def load_act(c, g, width):
+            t = keep.tile([P, 4, width], BF16, name="raw%d_%d" % (c, g), align_bytes=64)
+            nc.sync.dma_start(
+                out=t[:],
+                in_=act_basis[512 * g : 512 * (g + 1), W * c : W * c + width].rearrange("(p t) n -> p t n", t=4),
+            )
+            for i in range(width // W):
+                raw[(c + i, g)] = (t, W * i)
+
+        def load_mean(a, b):
+            nc.sync.dma_start(out=mean[:, a:b], in_=mean_shape[a:b].partition_broadcast(P))
+
+        load_idw(0, 2 * W)
+        load_mean(0, 2 * W)
+        load_act(0, 0, W)
+        load_act(0, 1, W)
+        load_idw(2, 2 * W)
+        for q in range(4):
+            nc.sync.dma_start(
+                out=exp[32 * q + 4 : 32 * q + 12, :].bitcast(I32),
+                in_=ex_scales[:, 4 * q : 4 * q + 4, :].bitcast(I32),
+            )
+        load_exw(0)
+        load_act(1, 0, W)
+        load_act(1, 1, W)
+        load_exw(1)
+        load_mean(2 * W, N)
+        load_idw(4, 2 * W)
+        load_act(2, 0, 2 * W)
+        load_act(2, 1, 2 * W)
+        load_exw(2)
+        load_exw(3)
+
+        ccode, cscale, cgrp = [], [], []
+        cbank = []
+        for m in range(MT):
+            bank = psum.tile([P, G, 2, P], F32, name="bank")
+            words = craw[m][:].bitcast(F32)
+            for g in range(G):
+                for u in range(2):
+                    nc.tensor.transpose(bank[:, g, u, :], words[:, 256 * g + u : 256 * (g + 1) : 2], ident[:])
+            cbank.append(bank)
+        for m in range(MT):
+            t = keep.tile([P, G, P, 4], BF16, name="cgrp%d" % m, align_bytes=64)
+            dst = t[:].rearrange("p g m t -> p (g m t)").bitcast(F32).rearrange("p (g m u) -> p g m u", g=G, u=2)
+            src = cbank[m][:].rearrange("p g u m -> p g m u")
+            if m % 2 == 0:
+                nc.scalar.copy(out=dst, in_=src)
+            else:
+                nc.vector.tensor_copy(out=dst, in_=src)
+            cgrp.append(t)
+            if m % 2 == 1:
+                for mm in (m - 1, m):
+                    cc = keep.tile([P, G, P], U32, name="ccode%d" % mm, align_bytes=64)
+                    cs = keep.tile([P, G, P], U8, name="cscale%d" % mm, align_bytes=64)
+                    nc.vector.quantize_mx(
+                        out=cc[:].rearrange("p g m -> p (g m)").bitcast(FP8X4),
+                        scales=cs[:].rearrange("p g m -> p (g m)"),
+                        in_=cgrp[mm][:].rearrange("p g m t -> p (g m t)"),
+                    )
+                    ccode.append(cc)
+                    cscale.append(cs)
+
+        grp = {}
+        acode, ascale = {}, {}
+        im = {}
+        bank_of = {}
+
+        def interleave(eng, c, g, a, b):
+            if (c, g) not in grp:
+                grp[(c, g)] = work.tile([P, W, 4], BF16, name="grp%d" % g, align_bytes=64)
+            t, off = raw[(c, g)]
+            src = t[:, :, off + a : off + b].rearrange("p t (c i) -> p c t i", i=4)
+            dst = grp[(c, g)][:, a:b, :].rearrange("p (c i) t -> p c t i", i=4)
+            if eng == "S":
+                nc.scalar.copy(out=dst, in_=src)
+            elif eng == "V":
+                nc.vector.tensor_copy(out=dst, in_=src)
+            else:
+                nc.gpsimd.tensor_scalar(out=dst, in0=src, scalar1=1.0, scalar2=0.0, op0=ALU.mult, op1=ALU.add)
+
+        def quantise(c, g):
+            cc = keep.tile([P, W], U32, name="acode%d_%d" % (c, g), align_bytes=64)
+            cs = keep.tile([P, W], U8, name="ascale%d_%d" % (c, g), align_bytes=64)
+            nc.vector.quantize_mx(out=cc[:].bitcast(FP8X4), scales=cs[:], in_=grp[(c, g)][:].rearrange("p n t -> p (n t)"))
+            acode[(c, g)] = cc
+            ascale[(c, g)] = cs
+
+        def product(kind, c, m):
+            bank = psum.tile([P, W], F32, name="bank")
+            for g in range(G):
+                if kind == "id":
+                    t, off = idw[c]
+                    rhs = t[:, g, off : off + 2 * W].bitcast(FP4X4)
+                    rhs_scale = idp[:, g, W * c : W * (c + 1)]
+                elif kind == "ex":
+                    rhs = exw[c][:, g, :].bitcast(FP8X4)
+                    rhs_scale = exp[4 + 4 * g : P, W * c : W * (c + 1)]
+                else:
+                    rhs = acode[(c, g)][:].bitcast(FP8X4)
+                    rhs_scale = ascale[(c, g)][:]
+                nc.tensor.matmul_mx(
+                    out=bank[:],
+                    lhsT=ccode[m][:, g, :].bitcast(FP8X4),
+                    lhsT_scale=cscale[m][:, g, :],
+                    rhs=rhs,
+                    rhs_scale=rhs_scale,
+                    start=(g == 0),
+                    stop=(g == G - 1),
+                )
+            bank_of[(kind, c, m)] = bank
+
+        def ident_exit(c, m, eng):
+            t = work.tile([P, W], F32, name="im", bufs=14)
+            mu = mean[:, W * c : W * (c + 1)]
+            bank = bank_of[("id", c, m)]
+            if eng == "V":
+                nc.vector.tensor_tensor(out=t[:], in0=bank[:], in1=mu, op=ALU.add)
+            else:
+                nc.scalar.copy(out=t[:], in_=bank[:])
+                nc.gpsimd.tensor_tensor(out=t[:], in0=t[:], in1=mu, op=ALU.add)
+            im[(c, m)] = t
+
+        th = {}
+
+        def tanh(c, m):
+            t = work.tile([P, W], F32, name="th")
+            nc.scalar.activation(out=t[:], in_=bank_of[("act", c, m)][:], func=ACT.Tanh)
+            th[(c, m)] = t
+
+        ob = {}
+
+        def mul(c, m):
+            t = work.tile([P, W], F32, name="ob", bufs=6)
+            nc.vector.tensor_tensor(out=t[:], in0=bank_of[("ex", c, m)][:], in1=th[(c, m)][:], op=ALU.mult)
+            ob[(c, m)] = t
+
+        def finish(c, m, eng):
+            t = ob[(c, m)]
+            e = nc.vector if eng == "V" else nc.gpsimd
+            e.tensor_tensor(out=t[:], in0=t[:], in1=im[(c, m)][:], op=ALU.add)
+            nc.sync.dma_start(out=out[m * P : (m + 1) * P, W * c : W * (c + 1)], in_=t[:])
+
+        order = [(i // MT, i % MT) for i in range(CHUNKS * MT)]
+        head_s = (1, 4, 7, 10)
+        for i in range(12):
+            product("id", *order[i])
+            ident_exit(*order[i], "S" if i in head_s else "V")
+            if i == 5:
+                for g in range(G):
+                    interleave("S", 0, g, 0, 256)
+                    interleave("V", 0, g, 256, 512)
+                quantise(0, 0)
+            if i == 7:
+                quantise(0, 1)
+        interleave("G", 1, 0, 256, 512)
+        interleave("S", 1, 0, 0, 256)
+        interleave("G", 1, 1, 0, 192)
+        interleave("V", 1, 1, 192, 320)
+        interleave("S", 1, 1, 320, 512)
+
+        ident_steps = (0, 2, 4, 5, 7, 9, 10, 12, 14, 15, 17, 19)
+        nxt = 12
+        for q in range(CHUNKS * MT):
+            c, m = order[q]
+            product("act", c, m)
+            tanh(c, m)
+            product("ex", c, m)
+            if q in ident_steps:
+                product("id", *order[nxt])
+            if q > 0:
+                mul(*order[q - 1])
+                finish(*order[q - 1], "G")
+            if q in ident_steps:
+                ident_exit(*order[nxt], "V")
+                nxt += 1
+            if q == 1:
+                load_act(4, 0, 2 * W)
+            if q == 2:
+                load_act(4, 1, 2 * W)
+            if q == 3:
+                load_exw(4)
+                load_exw(5)
+            if c + 2 < CHUNKS:
+                interleave("S", c + 2, 0, 128 * m, 128 * (m + 1))
+                if m == 2:
+                    interleave("V", c + 2, 1, 0, 320)
+                if m == 3:
+                    interleave("S", c + 2, 1, 320, 512)
+            if c + 1 < CHUNKS:
+                if m == 0:
+                    quantise(c + 1, 0)
+                if m == 1:
+                    quantise(c + 1, 1)
+        mul(*order[-1])
+        finish(*order[-1], "V")

@@ -31,27 +31,30 @@ def tile_morphable_face_decode_s10_kernel(tc, code, id_words, id_scales, ex_word
         psum = ctx.enter_context(tc.psum_pool(name="psum", bufs=8))
         ctx.enter_context(tc.manual_schedule())
 
-        one = keep.tile([P, 1], F32, name="one")
-        nc.gpsimd.memset(one[:], 0.0)
-        warm = keep.tile([P, 1], F32, name="warm")
-        nc.scalar.activation(out=warm[:], in_=one[:], func=ACT.Tanh)
+        mrow = keep.tile([P, P], BF16, name="mrow", align_bytes=64)
+        nc.vector.memset(mrow[:].bitcast(I32), 0)
         ident = keep.tile([P, P], F32, name="ident")
         make_identity(nc, ident[:])
         idp = keep.tile([P, G, N], U8, name="idp", align_bytes=64)
         nc.vector.memset(idp[:].rearrange("p g n -> p (g n)").bitcast(I32), 0)
+        identb = keep.tile([P, P], BF16, name="identb")
         exp = keep.tile([P, N], U8, name="exp", align_bytes=64)
         nc.vector.memset(exp[:].bitcast(I32), 0)
+        nc.vector.tensor_copy(out=identb[:], in_=ident[:])
 
         craw = []
-        for m in range(MT):
-            t = keep.tile([P, K], BF16, name="craw%d" % m, align_bytes=64)
-            nc.sync.dma_start(out=t[:], in_=code[m * P : (m + 1) * P, :])
-            craw.append(t)
+        for m0, count in ((0, 1), (1, 1), (2, 2)):
+            t = keep.tile([P, count, K], BF16, name="craw%d" % m0, align_bytes=64)
+            nc.sync.dma_start(out=t[:], in_=code[m0 * P : (m0 + count) * P, :].rearrange("(m p) k -> p m k", p=P))
+            craw.extend((t, i) for i in range(count))
+        nc.scalar.dma_start(out=mrow[0 : N // P, :], in_=mean_shape.rearrange("(c p) -> c p", p=P))
         for q in range(4):
-            nc.sync.dma_start(
+            nc.scalar.dma_start(
                 out=idp[32 * q : 32 * q + 4, :, :].bitcast(I32),
                 in_=id_scales[:, 4 * q : 4 * q + 4, :].rearrange("g r n -> r g n").bitcast(I32),
             )
+        warm = keep.tile([P, 1], F32, name="warm")
+        nc.scalar.activation(out=warm[:], in_=ident[:, 0:1], func=ACT.Tanh)
         mean = keep.tile([P, N], BF16, name="mean", align_bytes=64)
         idw = {}
         exw = {}
@@ -83,40 +86,49 @@ def tile_morphable_face_decode_s10_kernel(tc, code, id_words, id_scales, ex_word
             for i in range(width // W):
                 raw[(c + i, g)] = (t, W * i)
 
-        def load_mean(a, b):
-            nc.sync.dma_start(out=mean[:, a:b], in_=mean_shape[a:b].partition_broadcast(P))
+        def load_exs():
+            for q in range(4):
+                nc.sync.dma_start(
+                    out=exp[32 * q + 4 : 32 * q + 12, :].bitcast(I32),
+                    in_=ex_scales[:, 4 * q : 4 * q + 4, :].bitcast(I32),
+                )
 
-        load_idw(0, 2 * W)
-        load_mean(0, 2 * W)
+        load_idw(0, W)
+        load_idw(1, W)
         load_act(0, 0, W)
         load_act(0, 1, W)
         load_idw(2, 2 * W)
-        for q in range(4):
-            nc.sync.dma_start(
-                out=exp[32 * q + 4 : 32 * q + 12, :].bitcast(I32),
-                in_=ex_scales[:, 4 * q : 4 * q + 4, :].bitcast(I32),
-            )
+        load_exs()
         load_exw(0)
         load_act(1, 0, W)
         load_act(1, 1, W)
         load_exw(1)
-        load_mean(2 * W, N)
-        load_idw(4, 2 * W)
         load_act(2, 0, 2 * W)
         load_act(2, 1, 2 * W)
+        load_idw(4, 2 * W)
         load_exw(2)
         load_exw(3)
 
-        ccode, cscale, cgrp = [], [], []
+        def mean_spread(i):
+            bank = psum.tile([P, 2 * W], BF16, name="bank")
+            for j in range(2 * W // P):
+                c = i * (2 * W // P) + j
+                nc.tensor.transpose(bank[:, P * j : P * (j + 1)], mcol[:, c : c + 1].to_broadcast([P, P]), identb[:])
+            nc.scalar.copy(out=mean[:, 2 * W * i : 2 * W * (i + 1)], in_=bank[:])
+
+        ccode, cscale = [], []
         cbank = []
-        for m in range(MT):
+
+        def code_transpose(m):
             bank = psum.tile([P, G, 2, P], F32, name="bank")
-            words = craw[m][:].bitcast(F32)
+            t, i = craw[m]
+            words = t[:, i, :].bitcast(F32)
             for g in range(G):
                 for u in range(2):
                     nc.tensor.transpose(bank[:, g, u, :], words[:, 256 * g + u : 256 * (g + 1) : 2], ident[:])
             cbank.append(bank)
-        for m in range(MT):
+
+        def code_quantise(m):
             t = keep.tile([P, G, P, 4], BF16, name="cgrp%d" % m, align_bytes=64)
             dst = t[:].rearrange("p g m t -> p (g m t)").bitcast(F32).rearrange("p (g m u) -> p g m u", g=G, u=2)
             src = cbank[m][:].rearrange("p g u m -> p g m u")
@@ -124,18 +136,29 @@ def tile_morphable_face_decode_s10_kernel(tc, code, id_words, id_scales, ex_word
                 nc.scalar.copy(out=dst, in_=src)
             else:
                 nc.vector.tensor_copy(out=dst, in_=src)
-            cgrp.append(t)
-            if m % 2 == 1:
-                for mm in (m - 1, m):
-                    cc = keep.tile([P, G, P], U32, name="ccode%d" % mm, align_bytes=64)
-                    cs = keep.tile([P, G, P], U8, name="cscale%d" % mm, align_bytes=64)
-                    nc.vector.quantize_mx(
-                        out=cc[:].rearrange("p g m -> p (g m)").bitcast(FP8X4),
-                        scales=cs[:].rearrange("p g m -> p (g m)"),
-                        in_=cgrp[mm][:].rearrange("p g m t -> p (g m t)"),
-                    )
-                    ccode.append(cc)
-                    cscale.append(cs)
+            cc = keep.tile([P, G, P], U32, name="ccode%d" % m, align_bytes=64)
+            cs = keep.tile([P, G, P], U8, name="cscale%d" % m, align_bytes=64)
+            nc.vector.quantize_mx(
+                out=cc[:].rearrange("p g m -> p (g m)").bitcast(FP8X4),
+                scales=cs[:].rearrange("p g m -> p (g m)"),
+                in_=t[:].rearrange("p g m t -> p (g m t)"),
+            )
+            ccode.append(cc)
+            cscale.append(cs)
+
+        code_transpose(0)
+        code_transpose(1)
+        mbank = psum.tile([P, P], BF16, name="bank")
+        nc.tensor.transpose(mbank[:], mrow[:], identb[:])
+        mcol = keep.tile([P, CHUNKS * MT], BF16, name="mcol")
+        nc.vector.tensor_copy(out=mcol[:], in_=mbank[:, 0 : CHUNKS * MT])
+        code_quantise(0)
+        code_quantise(1)
+        mean_spread(0)
+        code_transpose(2)
+        code_transpose(3)
+        code_quantise(2)
+        code_quantise(3)
 
         grp = {}
         acode, ascale = {}, {}
@@ -207,7 +230,7 @@ def tile_morphable_face_decode_s10_kernel(tc, code, id_words, id_scales, ex_word
         ob = {}
 
         def mul(c, m):
-            t = work.tile([P, W], F32, name="ob", bufs=6)
+            t = work.tile([P, W], F32, name="ob", bufs=9)
             nc.vector.tensor_tensor(out=t[:], in0=bank_of[("ex", c, m)][:], in1=th[(c, m)][:], op=ALU.mult)
             ob[(c, m)] = t
 
@@ -217,56 +240,223 @@ def tile_morphable_face_decode_s10_kernel(tc, code, id_words, id_scales, ex_word
             e.tensor_tensor(out=t[:], in0=t[:], in1=im[(c, m)][:], op=ALU.add)
             nc.sync.dma_start(out=out[m * P : (m + 1) * P, W * c : W * (c + 1)], in_=t[:])
 
-        order = [(i // MT, i % MT) for i in range(CHUNKS * MT)]
-        head_s = (1, 4, 7, 10)
-        for i in range(12):
-            product("id", *order[i])
-            ident_exit(*order[i], "S" if i in head_s else "V")
-            if i == 5:
-                for g in range(G):
-                    interleave("S", 0, g, 0, 256)
-                    interleave("V", 0, g, 256, 512)
-                quantise(0, 0)
-            if i == 7:
-                quantise(0, 1)
-        interleave("G", 1, 0, 256, 512)
+        product("id", 0,0)
+        ident_exit(0,0, "V")
+        product("id", 0,1)
+        ident_exit(0,1, "S")
+        product("id", 0,2)
+        ident_exit(0,2, "V")
+        product("id", 0,3)
+        ident_exit(0,3, "S")
+        mean_spread(1)
+        product("id", 1,0)
+        ident_exit(1,0, "V")
+        mean_spread(2)
+        product("id", 1,1)
+        ident_exit(1,1, "S")
+        interleave("S", 0, 0, 0, 224)
+        interleave("V", 0, 0, 224, 512)
+        interleave("S", 0, 1, 0, 224)
+        interleave("V", 0, 1, 224, 512)
+        product("id", 1,2)
+        ident_exit(1,2, "V")
+        quantise(0, 0)
+        product("id", 1,3)
+        ident_exit(1,3, "S")
+        quantise(0, 1)
+        product("id", 2,0)
+        ident_exit(2,0, "V")
         interleave("S", 1, 0, 0, 256)
-        interleave("G", 1, 1, 0, 192)
-        interleave("V", 1, 1, 192, 320)
-        interleave("S", 1, 1, 320, 512)
-
-        ident_steps = (0, 2, 4, 5, 7, 9, 10, 12, 14, 15, 17, 19)
-        nxt = 12
-        for q in range(CHUNKS * MT):
-            c, m = order[q]
-            product("act", c, m)
-            tanh(c, m)
-            product("ex", c, m)
-            if q in ident_steps:
-                product("id", *order[nxt])
-            if q > 0:
-                mul(*order[q - 1])
-                finish(*order[q - 1], "G")
-            if q in ident_steps:
-                ident_exit(*order[nxt], "V")
-                nxt += 1
-            if q == 1:
-                load_act(4, 0, 2 * W)
-            if q == 2:
-                load_act(4, 1, 2 * W)
-            if q == 3:
-                load_exw(4)
-                load_exw(5)
-            if c + 2 < CHUNKS:
-                interleave("S", c + 2, 0, 128 * m, 128 * (m + 1))
-                if m == 2:
-                    interleave("V", c + 2, 1, 0, 320)
-                if m == 3:
-                    interleave("S", c + 2, 1, 320, 512)
-            if c + 1 < CHUNKS:
-                if m == 0:
-                    quantise(c + 1, 0)
-                if m == 1:
-                    quantise(c + 1, 1)
-        mul(*order[-1])
-        finish(*order[-1], "V")
+        interleave("G", 1, 0, 256, 384)
+        interleave("V", 1, 0, 384, 512)
+        product("id", 2,1)
+        ident_exit(2,1, "S")
+        product("id", 2,2)
+        ident_exit(2,2, "V")
+        interleave("S", 1, 1, 0, 256)
+        interleave("G", 1, 1, 256, 384)
+        interleave("V", 1, 1, 384, 512)
+        product("id", 2,3)
+        ident_exit(2,3, "S")
+        product("act", 0, 0)
+        tanh(0, 0)
+        product("ex", 0, 0)
+        product("id", 3,0)
+        ident_exit(3,0, "V")
+        interleave("S", 2, 0, 0, 128)
+        quantise(1, 0)
+        product("act", 0, 1)
+        tanh(0, 1)
+        product("ex", 0, 1)
+        mul(0,0)
+        finish(0,0, "G")
+        load_act(4, 0, 2 * W)
+        interleave("S", 2, 0, 128, 256)
+        quantise(1, 1)
+        product("act", 0, 2)
+        tanh(0, 2)
+        product("ex", 0, 2)
+        product("id", 3,1)
+        mul(0,1)
+        finish(0,1, "G")
+        ident_exit(3,1, "V")
+        load_act(4, 1, 2 * W)
+        interleave("S", 2, 0, 256, 384)
+        interleave("V", 2, 1, 0, 320)
+        product("act", 0, 3)
+        tanh(0, 3)
+        product("ex", 0, 3)
+        mul(0,2)
+        finish(0,2, "G")
+        load_exw(4)
+        load_exw(5)
+        interleave("S", 2, 0, 384, 512)
+        interleave("S", 2, 1, 320, 512)
+        product("act", 1, 0)
+        tanh(1, 0)
+        product("ex", 1, 0)
+        product("id", 3,2)
+        mul(0,3)
+        finish(0,3, "G")
+        ident_exit(3,2, "V")
+        interleave("S", 3, 0, 0, 128)
+        quantise(2, 0)
+        product("act", 1, 1)
+        tanh(1, 1)
+        product("ex", 1, 1)
+        product("id", 3,3)
+        mul(1,0)
+        finish(1,0, "G")
+        ident_exit(3,3, "V")
+        interleave("S", 3, 0, 128, 256)
+        quantise(2, 1)
+        product("act", 1, 2)
+        tanh(1, 2)
+        product("ex", 1, 2)
+        mul(1,1)
+        finish(1,1, "G")
+        interleave("S", 3, 0, 256, 384)
+        interleave("V", 3, 1, 0, 320)
+        product("act", 1, 3)
+        tanh(1, 3)
+        product("ex", 1, 3)
+        product("id", 4,0)
+        mul(1,2)
+        finish(1,2, "G")
+        ident_exit(4,0, "V")
+        interleave("S", 3, 0, 384, 512)
+        interleave("S", 3, 1, 320, 512)
+        product("act", 2, 0)
+        tanh(2, 0)
+        product("ex", 2, 0)
+        mul(1,3)
+        finish(1,3, "G")
+        interleave("S", 4, 0, 0, 128)
+        quantise(3, 0)
+        product("act", 2, 1)
+        tanh(2, 1)
+        product("ex", 2, 1)
+        product("id", 4,1)
+        mul(2,0)
+        finish(2,0, "G")
+        ident_exit(4,1, "V")
+        interleave("S", 4, 0, 128, 256)
+        quantise(3, 1)
+        product("act", 2, 2)
+        tanh(2, 2)
+        product("ex", 2, 2)
+        product("id", 4,2)
+        mul(2,1)
+        finish(2,1, "G")
+        ident_exit(4,2, "V")
+        interleave("S", 4, 0, 256, 384)
+        interleave("V", 4, 1, 0, 320)
+        product("act", 2, 3)
+        tanh(2, 3)
+        product("ex", 2, 3)
+        mul(2,2)
+        finish(2,2, "G")
+        interleave("S", 4, 0, 384, 512)
+        interleave("S", 4, 1, 320, 512)
+        product("act", 3, 0)
+        tanh(3, 0)
+        product("ex", 3, 0)
+        product("id", 4,3)
+        mul(2,3)
+        finish(2,3, "G")
+        ident_exit(4,3, "V")
+        interleave("S", 5, 0, 0, 128)
+        quantise(4, 0)
+        product("act", 3, 1)
+        tanh(3, 1)
+        product("ex", 3, 1)
+        mul(3,0)
+        finish(3,0, "G")
+        interleave("S", 5, 0, 128, 256)
+        quantise(4, 1)
+        product("act", 3, 2)
+        tanh(3, 2)
+        product("ex", 3, 2)
+        product("id", 5,0)
+        mul(3,1)
+        finish(3,1, "G")
+        ident_exit(5,0, "V")
+        interleave("S", 5, 0, 256, 384)
+        interleave("V", 5, 1, 0, 320)
+        product("act", 3, 3)
+        tanh(3, 3)
+        product("ex", 3, 3)
+        product("id", 5,1)
+        mul(3,2)
+        finish(3,2, "G")
+        ident_exit(5,1, "V")
+        interleave("S", 5, 0, 384, 512)
+        interleave("S", 5, 1, 320, 512)
+        product("act", 4, 0)
+        tanh(4, 0)
+        product("ex", 4, 0)
+        mul(3,3)
+        finish(3,3, "G")
+        quantise(5, 0)
+        product("act", 4, 1)
+        tanh(4, 1)
+        product("ex", 4, 1)
+        product("id", 5,2)
+        mul(4,0)
+        finish(4,0, "G")
+        ident_exit(5,2, "V")
+        quantise(5, 1)
+        product("act", 4, 2)
+        tanh(4, 2)
+        product("ex", 4, 2)
+        mul(4,1)
+        finish(4,1, "G")
+        product("act", 4, 3)
+        tanh(4, 3)
+        product("ex", 4, 3)
+        product("id", 5,3)
+        mul(4,2)
+        finish(4,2, "G")
+        ident_exit(5,3, "V")
+        product("act", 5, 0)
+        tanh(5, 0)
+        product("ex", 5, 0)
+        mul(4,3)
+        finish(4,3, "G")
+        product("act", 5, 1)
+        tanh(5, 1)
+        product("ex", 5, 1)
+        mul(5,0)
+        finish(5,0, "V")
+        product("act", 5, 2)
+        tanh(5, 2)
+        product("ex", 5, 2)
+        mul(5,1)
+        finish(5,1, "V")
+        product("act", 5, 3)
+        tanh(5, 3)
+        product("ex", 5, 3)
+        mul(5,2)
+        finish(5,2, "V")
+        mul(5,3)
+        finish(5,3, "V")

@@ -33,32 +33,19 @@ def tile_morphable_face_decode_s10_kernel(tc, code, id_words, id_scales, ex_word
 
         mrow = keep.tile([P, P], BF16, name="mrow", align_bytes=64)
         nc.vector.memset(mrow[:].bitcast(I32), 0)
+        nc.gpsimd.dma_start(out=mrow[0 : N // P, :], in_=mean_shape.rearrange("(c p) -> c p", p=P))
         ident = keep.tile([P, P], F32, name="ident")
         make_identity(nc, ident[:])
-        idp = keep.tile([P, G, N], U8, name="idp", align_bytes=64)
-        nc.vector.memset(idp[:].rearrange("p g n -> p (g n)").bitcast(I32), 0)
-        identb = keep.tile([P, P], BF16, name="identb")
-        exp = keep.tile([P, N], U8, name="exp", align_bytes=64)
-        nc.vector.memset(exp[:].bitcast(I32), 0)
-        nc.vector.tensor_copy(out=identb[:], in_=ident[:])
-
-        craw = []
-        for m0, count in ((0, 1), (1, 1), (2, 2)):
-            t = keep.tile([P, count, K], BF16, name="craw%d" % m0, align_bytes=64)
-            nc.sync.dma_start(out=t[:], in_=code[m0 * P : (m0 + count) * P, :].rearrange("(m p) k -> p m k", p=P))
-            craw.extend((t, i) for i in range(count))
-        nc.scalar.dma_start(out=mrow[0 : N // P, :], in_=mean_shape.rearrange("(c p) -> c p", p=P))
-        for q in range(4):
-            nc.scalar.dma_start(
-                out=idp[32 * q : 32 * q + 4, :, :].bitcast(I32),
-                in_=id_scales[:, 4 * q : 4 * q + 4, :].rearrange("g r n -> r g n").bitcast(I32),
-            )
-        warm = keep.tile([P, 1], F32, name="warm")
-        nc.scalar.activation(out=warm[:], in_=ident[:, 0:1], func=ACT.Tanh)
-        mean = keep.tile([P, N], BF16, name="mean", align_bytes=64)
         idw = {}
         exw = {}
         raw = {}
+        idp = {}
+        craw = []
+
+        def load_code(m0, count):
+            t = keep.tile([P, count, K], BF16, name="craw%d" % m0, align_bytes=64)
+            nc.sync.dma_start(out=t[:], in_=code[m0 * P : (m0 + count) * P, :].rearrange("(m p) k -> p m k", p=P))
+            craw.extend((t, i) for i in range(count))
 
         def load_idw(c, width):
             t = keep.tile([P, G, 2 * width], U8, name="idw%d" % c, align_bytes=64)
@@ -69,6 +56,34 @@ def tile_morphable_face_decode_s10_kernel(tc, code, id_words, id_scales, ex_word
             for i in range(width // W):
                 idw[c + i] = (t, 2 * W * i)
 
+        def make_idp(c, count, eng):
+            t = keep.tile([P, G, count * W], U8, name="idp%d" % c, align_bytes=64)
+            eng.memset(t[:].rearrange("p g n -> p (g n)").bitcast(I32), 0)
+            for i in range(count):
+                idp[c + i] = (t, W * i)
+
+        def load_idp(c, count, eng):
+            t = idp[c][0]
+            for q in range(4):
+                eng.dma_start(
+                    out=t[32 * q : 32 * q + 4, :, :].bitcast(I32),
+                    in_=id_scales[:, 4 * q : 4 * q + 4, W * c : W * (c + count)].rearrange("g r n -> r g n").bitcast(I32),
+                )
+
+        make_idp(0, 2, nc.vector)
+        load_code(0, 1)
+        load_idw(0, W)
+        load_idp(0, 2, nc.scalar)
+        load_code(1, 1)
+        load_code(2, 2)
+        warm = keep.tile([P, 1], F32, name="warm")
+        nc.scalar.activation(out=warm[:], in_=ident[:, 0:1], func=ACT.Tanh)
+        identb = keep.tile([P, P], BF16, name="identb")
+        nc.vector.tensor_copy(out=identb[:], in_=ident[:])
+        make_idp(2, 4, nc.gpsimd)
+        exp = keep.tile([P, N], U8, name="exp", align_bytes=64)
+        nc.gpsimd.memset(exp[:].bitcast(I32), 0)
+        mean = keep.tile([P, N], BF16, name="mean", align_bytes=64)
         def load_exw(c):
             t = keep.tile([P, G, 4 * W], U8, name="exw%d" % c, align_bytes=64)
             nc.sync.dma_start(
@@ -86,6 +101,9 @@ def tile_morphable_face_decode_s10_kernel(tc, code, id_words, id_scales, ex_word
             for i in range(width // W):
                 raw[(c + i, g)] = (t, W * i)
 
+        def load_mean(a):
+            nc.sync.dma_start(out=mean[:, a:N], in_=mean_shape[a:N].partition_broadcast(P))
+
         def load_exs():
             for q in range(4):
                 nc.sync.dma_start(
@@ -93,31 +111,33 @@ def tile_morphable_face_decode_s10_kernel(tc, code, id_words, id_scales, ex_word
                     in_=ex_scales[:, 4 * q : 4 * q + 4, :].bitcast(I32),
                 )
 
-        load_idw(0, W)
         load_idw(1, W)
         load_act(0, 0, W)
         load_act(0, 1, W)
+        load_idp(2, 4, nc.sync)
         load_idw(2, 2 * W)
-        load_exs()
         load_exw(0)
+        load_exs()
         load_act(1, 0, W)
         load_act(1, 1, W)
+        load_act(2, 0, W)
+        load_act(2, 1, W)
         load_exw(1)
-        load_act(2, 0, 2 * W)
-        load_act(2, 1, 2 * W)
         load_idw(4, 2 * W)
-        load_exw(2)
-        load_exw(3)
+        load_act(3, 0, W)
+        load_act(3, 1, W)
 
-        def mean_spread(i):
-            bank = psum.tile([P, 2 * W], BF16, name="bank")
-            for j in range(2 * W // P):
-                c = i * (2 * W // P) + j
+        def mean_spread(a, b):
+            bank = psum.tile([P, b - a], BF16, name="bank")
+            for j in range((b - a) // P):
+                c = a // P + j
                 nc.tensor.transpose(bank[:, P * j : P * (j + 1)], mcol[:, c : c + 1].to_broadcast([P, P]), identb[:])
-            nc.scalar.copy(out=mean[:, 2 * W * i : 2 * W * (i + 1)], in_=bank[:])
+            mbanks[a // (2 * W)] = bank
 
-        ccode, cscale = [], []
-        cbank = []
+        def mean_copy(i):
+            nc.scalar.copy(out=mean[:, 2 * W * i : 2 * W * (i + 1)], in_=mbanks[i][:])
+
+        ccode, cscale, cgrp, cbank = {}, {}, {}, {}
 
         def code_transpose(m):
             bank = psum.tile([P, G, 2, P], F32, name="bank")
@@ -126,9 +146,9 @@ def tile_morphable_face_decode_s10_kernel(tc, code, id_words, id_scales, ex_word
             for g in range(G):
                 for u in range(2):
                     nc.tensor.transpose(bank[:, g, u, :], words[:, 256 * g + u : 256 * (g + 1) : 2], ident[:])
-            cbank.append(bank)
+            cbank[m] = bank
 
-        def code_quantise(m):
+        def code_copy(m):
             t = keep.tile([P, G, P, 4], BF16, name="cgrp%d" % m, align_bytes=64)
             dst = t[:].rearrange("p g m t -> p (g m t)").bitcast(F32).rearrange("p (g m u) -> p g m u", g=G, u=2)
             src = cbank[m][:].rearrange("p g u m -> p g m u")
@@ -136,6 +156,10 @@ def tile_morphable_face_decode_s10_kernel(tc, code, id_words, id_scales, ex_word
                 nc.scalar.copy(out=dst, in_=src)
             else:
                 nc.vector.tensor_copy(out=dst, in_=src)
+            cgrp[m] = t
+
+        def code_codes(m):
+            t = cgrp[m]
             cc = keep.tile([P, G, P], U32, name="ccode%d" % m, align_bytes=64)
             cs = keep.tile([P, G, P], U8, name="cscale%d" % m, align_bytes=64)
             nc.vector.quantize_mx(
@@ -143,22 +167,19 @@ def tile_morphable_face_decode_s10_kernel(tc, code, id_words, id_scales, ex_word
                 scales=cs[:].rearrange("p g m -> p (g m)"),
                 in_=t[:].rearrange("p g m t -> p (g m t)"),
             )
-            ccode.append(cc)
-            cscale.append(cs)
+            ccode[m] = cc
+            cscale[m] = cs
 
-        code_transpose(0)
-        code_transpose(1)
-        mbank = psum.tile([P, P], BF16, name="bank")
-        nc.tensor.transpose(mbank[:], mrow[:], identb[:])
         mcol = keep.tile([P, CHUNKS * MT], BF16, name="mcol")
-        nc.vector.tensor_copy(out=mcol[:], in_=mbank[:, 0 : CHUNKS * MT])
-        code_quantise(0)
-        code_quantise(1)
-        mean_spread(0)
-        code_transpose(2)
-        code_transpose(3)
-        code_quantise(2)
-        code_quantise(3)
+        mbanks = {}
+
+        def mean_column():
+            mbanks["col"] = psum.tile([P, P], BF16, name="bank")
+            nc.tensor.transpose(mbanks["col"][:], mrow[:], identb[:])
+
+        def mean_column_copy():
+            nc.vector.tensor_copy(out=mcol[:], in_=mbanks["col"][:, 0 : CHUNKS * MT])
+
 
         grp = {}
         acode, ascale = {}, {}
@@ -191,7 +212,8 @@ def tile_morphable_face_decode_s10_kernel(tc, code, id_words, id_scales, ex_word
                 if kind == "id":
                     t, off = idw[c]
                     rhs = t[:, g, off : off + 2 * W].bitcast(FP4X4)
-                    rhs_scale = idp[:, g, W * c : W * (c + 1)]
+                    sp, so = idp[c]
+                    rhs_scale = sp[:, g, so : so + W]
                 elif kind == "ex":
                     rhs = exw[c][:, g, :].bitcast(FP8X4)
                     rhs_scale = exp[4 + 4 * g : P, W * c : W * (c + 1)]
@@ -217,8 +239,11 @@ def tile_morphable_face_decode_s10_kernel(tc, code, id_words, id_scales, ex_word
                 nc.vector.tensor_tensor(out=t[:], in0=bank[:], in1=mu, op=ALU.add)
             else:
                 nc.scalar.copy(out=t[:], in_=bank[:])
-                nc.gpsimd.tensor_tensor(out=t[:], in0=t[:], in1=mu, op=ALU.add)
             im[(c, m)] = t
+
+        def ident_mean(c, m):
+            t = im[(c, m)]
+            nc.gpsimd.tensor_tensor(out=t[:], in0=t[:], in1=mean[:, W * c : W * (c + 1)], op=ALU.add)
 
         th = {}
 
@@ -228,6 +253,19 @@ def tile_morphable_face_decode_s10_kernel(tc, code, id_words, id_scales, ex_word
             th[(c, m)] = t
 
         ob = {}
+
+        def last_tile(c, m, parts):
+            mu = mean[:, W * c : W * (c + 1)]
+            t = work.tile([P, W], F32, name="ob", bufs=9)
+            nc.vector.tensor_tensor(out=t[:], in0=bank_of[("ex", c, m)][:], in1=th[(c, m)][:], op=ALU.mult)
+            nc.vector.tensor_tensor(out=t[:], in0=t[:], in1=mu, op=ALU.add)
+            product("id", c, m)
+            bank = bank_of[("id", c, m)]
+            for i in range(parts):
+                cols = slice(W // parts * i, W // parts * (i + 1))
+                o = work.tile([P, W // parts], F32, name="lob", bufs=2)
+                nc.vector.tensor_tensor(out=o[:], in0=bank[:, cols], in1=t[:, cols], op=ALU.add)
+                nc.sync.dma_start(out=out[m * P : (m + 1) * P, W * c + cols.start : W * c + cols.stop], in_=o[:])
 
         def mul(c, m):
             t = work.tile([P, W], F32, name="ob", bufs=9)
@@ -240,223 +278,233 @@ def tile_morphable_face_decode_s10_kernel(tc, code, id_words, id_scales, ex_word
             e.tensor_tensor(out=t[:], in0=t[:], in1=im[(c, m)][:], op=ALU.add)
             nc.sync.dma_start(out=out[m * P : (m + 1) * P, W * c : W * (c + 1)], in_=t[:])
 
-        product("id", 0,0)
-        ident_exit(0,0, "V")
-        product("id", 0,1)
-        ident_exit(0,1, "S")
-        product("id", 0,2)
-        ident_exit(0,2, "V")
-        product("id", 0,3)
-        ident_exit(0,3, "S")
-        mean_spread(1)
-        product("id", 1,0)
-        ident_exit(1,0, "V")
-        mean_spread(2)
-        product("id", 1,1)
-        ident_exit(1,1, "S")
-        interleave("S", 0, 0, 0, 224)
-        interleave("V", 0, 0, 224, 512)
-        interleave("S", 0, 1, 0, 224)
-        interleave("V", 0, 1, 224, 512)
-        product("id", 1,2)
-        ident_exit(1,2, "V")
+        code_transpose(0)
+        mean_column()
+        code_copy(0)
+        mean_column_copy()
+        code_codes(0)
+        code_transpose(1)
+        mean_spread(0, 2 * W)
+        code_copy(1)
+        mean_copy(0)
+        code_transpose(2)
+        code_codes(1)
+        code_transpose(3)
+        code_copy(2)
+        product("id", 0, 0)
+        code_copy(3)
+        code_codes(2)
+        interleave("S", 0, 0, 0, 256)
+        code_codes(3)
+        product("id", 0, 1)
+        ident_exit(0, 0, "V")
+        interleave("V", 0, 0, 256, 512)
+        product("id", 0, 2)
+        interleave("S", 0, 1, 0, 256)
+        ident_exit(0, 1, "V")
         quantise(0, 0)
-        product("id", 1,3)
-        ident_exit(1,3, "S")
+        product("id", 0, 3)
+        interleave("S", 0, 1, 256, 512)
+        ident_exit(0, 2, "V")
+        mean_spread(2 * W, 4 * W)
+        ident_exit(0, 3, "V")
+        product("id", 1, 0)
+        mean_copy(1)
         quantise(0, 1)
-        product("id", 2,0)
-        ident_exit(2,0, "V")
-        interleave("S", 1, 0, 0, 256)
-        interleave("G", 1, 0, 256, 384)
-        interleave("V", 1, 0, 384, 512)
-        product("id", 2,1)
-        ident_exit(2,1, "S")
-        product("id", 2,2)
-        ident_exit(2,2, "V")
-        interleave("S", 1, 1, 0, 256)
-        interleave("G", 1, 1, 256, 384)
-        interleave("V", 1, 1, 384, 512)
-        product("id", 2,3)
-        ident_exit(2,3, "S")
+        ident_exit(1, 0, "V")
         product("act", 0, 0)
-        tanh(0, 0)
         product("ex", 0, 0)
-        product("id", 3,0)
-        ident_exit(3,0, "V")
-        interleave("S", 2, 0, 0, 128)
-        quantise(1, 0)
+        tanh(0, 0)
         product("act", 0, 1)
-        tanh(0, 1)
+        interleave("S", 1, 0, 0, 256)
+        mul(0, 0)
         product("ex", 0, 1)
-        mul(0,0)
-        finish(0,0, "G")
-        load_act(4, 0, 2 * W)
-        interleave("S", 2, 0, 128, 256)
-        quantise(1, 1)
+        interleave("V", 1, 0, 256, 512)
+        product("id", 1, 1)
+        tanh(0, 1)
+        interleave("V", 1, 1, 0, 256)
         product("act", 0, 2)
-        tanh(0, 2)
+        interleave("S", 1, 1, 256, 512)
+        quantise(1, 0)
         product("ex", 0, 2)
-        product("id", 3,1)
-        mul(0,1)
-        finish(0,1, "G")
-        ident_exit(3,1, "V")
-        load_act(4, 1, 2 * W)
-        interleave("S", 2, 0, 256, 384)
-        interleave("V", 2, 1, 0, 320)
+        mul(0, 1)
+        finish(0, 0, "G")
+        product("id", 1, 2)
+        tanh(0, 2)
+        ident_exit(1, 1, "V")
         product("act", 0, 3)
-        tanh(0, 3)
         product("ex", 0, 3)
-        mul(0,2)
-        finish(0,2, "G")
-        load_exw(4)
-        load_exw(5)
-        interleave("S", 2, 0, 384, 512)
-        interleave("S", 2, 1, 320, 512)
+        interleave("S", 2, 0, 0, 256)
+        mul(0, 2)
+        finish(0, 1, "G")
+        product("id", 1, 3)
+        ident_exit(1, 2, "V")
+        mean_spread(4 * W, 6 * W)
+        finish(0, 2, "G")
+        load_exw(2)
+        ident_exit(1, 3, "V")
+        tanh(0, 3)
+        interleave("S", 2, 0, 256, 512)
+        product("id", 2, 0)
+        mul(0, 3)
+        product("id", 2, 1)
+        quantise(1, 1)
+        mean_copy(2)
+        ident_exit(2, 0, "V")
+        finish(0, 3, "G")
+        load_exw(3)
         product("act", 1, 0)
-        tanh(1, 0)
+        interleave("S", 2, 1, 0, 256)
+        ident_exit(2, 1, "V")
         product("ex", 1, 0)
-        product("id", 3,2)
-        mul(0,3)
-        finish(0,3, "G")
-        ident_exit(3,2, "V")
-        interleave("S", 3, 0, 0, 128)
-        quantise(2, 0)
         product("act", 1, 1)
-        tanh(1, 1)
+        quantise(2, 0)
         product("ex", 1, 1)
-        product("id", 3,3)
-        mul(1,0)
-        finish(1,0, "G")
-        ident_exit(3,3, "V")
-        interleave("S", 3, 0, 128, 256)
-        quantise(2, 1)
+        tanh(1, 0)
+        interleave("V", 2, 1, 256, 512)
         product("act", 1, 2)
-        tanh(1, 2)
+        tanh(1, 1)
+        mul(1, 0)
         product("ex", 1, 2)
-        mul(1,1)
-        finish(1,1, "G")
-        interleave("S", 3, 0, 256, 384)
-        interleave("V", 3, 1, 0, 320)
+        tanh(1, 2)
+        quantise(2, 1)
+        product("id", 2, 2)
+        mul(1, 1)
+        finish(1, 0, "G")
+        load_act(4, 0, 2 * W)
         product("act", 1, 3)
-        tanh(1, 3)
+        mul(1, 2)
         product("ex", 1, 3)
-        product("id", 4,0)
-        mul(1,2)
-        finish(1,2, "G")
-        ident_exit(4,0, "V")
-        interleave("S", 3, 0, 384, 512)
-        interleave("S", 3, 1, 320, 512)
+        interleave("S", 3, 0, 0, 256)
+        ident_exit(2, 2, "V")
+        finish(1, 1, "G")
+        load_act(4, 1, 2 * W)
+        product("id", 2, 3)
         product("act", 2, 0)
-        tanh(2, 0)
+        ident_exit(2, 3, "V")
+        tanh(1, 3)
+        finish(1, 2, "G")
+        load_exw(4)
         product("ex", 2, 0)
-        mul(1,3)
-        finish(1,3, "G")
-        interleave("S", 4, 0, 0, 128)
-        quantise(3, 0)
+        tanh(2, 0)
+        mul(1, 3)
+        product("id", 3, 0)
+        interleave("S", 3, 0, 256, 512)
+        mul(2, 0)
+        finish(1, 3, "G")
+        load_exw(5)
         product("act", 2, 1)
-        tanh(2, 1)
+        ident_exit(3, 0, "V")
         product("ex", 2, 1)
-        product("id", 4,1)
-        mul(2,0)
-        finish(2,0, "G")
-        ident_exit(4,1, "V")
-        interleave("S", 4, 0, 128, 256)
-        quantise(3, 1)
+        tanh(2, 1)
+        finish(2, 0, "G")
+        product("id", 3, 1)
+        interleave("S", 3, 1, 0, 256)
+        mul(2, 1)
         product("act", 2, 2)
-        tanh(2, 2)
+        ident_exit(3, 1, "V")
+        finish(2, 1, "G")
         product("ex", 2, 2)
-        product("id", 4,2)
-        mul(2,1)
-        finish(2,1, "G")
-        ident_exit(4,2, "V")
-        interleave("S", 4, 0, 256, 384)
-        interleave("V", 4, 1, 0, 320)
+        tanh(2, 2)
+        product("id", 3, 2)
+        interleave("S", 3, 1, 256, 512)
+        mul(2, 2)
         product("act", 2, 3)
-        tanh(2, 3)
         product("ex", 2, 3)
-        mul(2,2)
-        finish(2,2, "G")
-        interleave("S", 4, 0, 384, 512)
-        interleave("S", 4, 1, 320, 512)
+        quantise(3, 0)
+        product("id", 3, 3)
+        tanh(2, 3)
+        ident_exit(3, 2, "V")
+        finish(2, 2, "G")
+        product("id", 4, 0)
+        interleave("S", 4, 0, 0, 256)
+        ident_exit(3, 3, "V")
+        product("id", 4, 1)
+        mul(2, 3)
+        product("id", 4, 2)
+        quantise(3, 1)
+        interleave("S", 4, 0, 256, 512)
+        ident_exit(4, 0, "V")
+        finish(2, 3, "G")
         product("act", 3, 0)
-        tanh(3, 0)
+        ident_exit(4, 1, "V")
         product("ex", 3, 0)
-        product("id", 4,3)
-        mul(2,3)
-        finish(2,3, "G")
-        ident_exit(4,3, "V")
-        interleave("S", 5, 0, 0, 128)
-        quantise(4, 0)
+        tanh(3, 0)
+        ident_exit(4, 2, "V")
         product("act", 3, 1)
-        tanh(3, 1)
+        interleave("S", 4, 1, 0, 256)
+        mul(3, 0)
         product("ex", 3, 1)
-        mul(3,0)
-        finish(3,0, "G")
-        interleave("S", 5, 0, 128, 256)
-        quantise(4, 1)
+        quantise(4, 0)
         product("act", 3, 2)
-        tanh(3, 2)
+        tanh(3, 1)
         product("ex", 3, 2)
-        product("id", 5,0)
-        mul(3,1)
-        finish(3,1, "G")
-        ident_exit(5,0, "V")
-        interleave("S", 5, 0, 256, 384)
-        interleave("V", 5, 1, 0, 320)
+        interleave("V", 4, 1, 256, 512)
+        tanh(3, 2)
         product("act", 3, 3)
-        tanh(3, 3)
+        mul(3, 1)
+        finish(3, 0, "G")
         product("ex", 3, 3)
-        product("id", 5,1)
-        mul(3,2)
-        finish(3,2, "G")
-        ident_exit(5,1, "V")
-        interleave("S", 5, 0, 384, 512)
-        interleave("S", 5, 1, 320, 512)
-        product("act", 4, 0)
-        tanh(4, 0)
-        product("ex", 4, 0)
-        mul(3,3)
-        finish(3,3, "G")
+        interleave("S", 5, 0, 0, 256)
+        mul(3, 2)
+        product("id", 4, 3)
+        finish(3, 1, "G")
+        product("id", 5, 0)
+        ident_exit(4, 3, "V")
+        tanh(3, 3)
+        product("id", 5, 1)
+        ident_exit(5, 0, "V")
+        interleave("S", 5, 0, 256, 512)
+        finish(3, 2, "G")
+        product("id", 5, 2)
+        mul(3, 3)
+        product("id", 5, 3)
+        ident_exit(5, 1, "V")
+        interleave("S", 5, 1, 0, 256)
+        finish(3, 3, "G")
+        ident_exit(5, 2, "V")
+        ident_exit(5, 3, "V")
+        interleave("S", 5, 1, 256, 512)
+        quantise(4, 1)
         quantise(5, 0)
-        product("act", 4, 1)
-        tanh(4, 1)
-        product("ex", 4, 1)
-        product("id", 5,2)
-        mul(4,0)
-        finish(4,0, "G")
-        ident_exit(5,2, "V")
+        product("act", 4, 0)
         quantise(5, 1)
+        product("ex", 4, 0)
+        tanh(4, 0)
+        product("act", 4, 1)
+        mul(4, 0)
+        product("ex", 4, 1)
+        tanh(4, 1)
+        finish(4, 0, "G")
         product("act", 4, 2)
-        tanh(4, 2)
+        mul(4, 1)
         product("ex", 4, 2)
-        mul(4,1)
-        finish(4,1, "G")
+        tanh(4, 2)
+        finish(4, 1, "G")
         product("act", 4, 3)
-        tanh(4, 3)
+        mul(4, 2)
         product("ex", 4, 3)
-        product("id", 5,3)
-        mul(4,2)
-        finish(4,2, "G")
-        ident_exit(5,3, "V")
+        tanh(4, 3)
+        finish(4, 2, "G")
         product("act", 5, 0)
-        tanh(5, 0)
+        mul(4, 3)
         product("ex", 5, 0)
-        mul(4,3)
-        finish(4,3, "G")
+        tanh(5, 0)
+        finish(4, 3, "G")
         product("act", 5, 1)
-        tanh(5, 1)
+        mul(5, 0)
         product("ex", 5, 1)
-        mul(5,0)
-        finish(5,0, "V")
+        tanh(5, 1)
+        finish(5, 0, "G")
         product("act", 5, 2)
-        tanh(5, 2)
+        mul(5, 1)
         product("ex", 5, 2)
-        mul(5,1)
-        finish(5,1, "V")
+        tanh(5, 2)
         product("act", 5, 3)
-        tanh(5, 3)
+        finish(5, 1, "G")
+        mul(5, 2)
         product("ex", 5, 3)
-        mul(5,2)
-        finish(5,2, "V")
-        mul(5,3)
-        finish(5,3, "V")
+        tanh(5, 3)
+        finish(5, 2, "V")
+        mul(5, 3)
+        finish(5, 3, "V")

@@ -126,6 +126,8 @@ def tile_morphable_face_decode_s10_kernel(tc, code, id_words, id_scales, ex_word
         load_idw(4, 2 * W)
         load_act(3, 0, W)
         load_act(3, 1, W)
+        load_exw(2)
+        load_exw(3)
 
         def mean_spread(a, b):
             bank = psum.tile([P, b - a], BF16, name="bank")
@@ -148,11 +150,11 @@ def tile_morphable_face_decode_s10_kernel(tc, code, id_words, id_scales, ex_word
                     nc.tensor.transpose(bank[:, g, u, :], words[:, 256 * g + u : 256 * (g + 1) : 2], ident[:])
             cbank[m] = bank
 
-        def code_copy(m):
+        def code_copy(m, eng):
             t = keep.tile([P, G, P, 4], BF16, name="cgrp%d" % m, align_bytes=64)
             dst = t[:].rearrange("p g m t -> p (g m t)").bitcast(F32).rearrange("p (g m u) -> p g m u", g=G, u=2)
             src = cbank[m][:].rearrange("p g u m -> p g m u")
-            if m % 2 == 0:
+            if eng == "S":
                 nc.scalar.copy(out=dst, in_=src)
             else:
                 nc.vector.tensor_copy(out=dst, in_=src)
@@ -232,7 +234,7 @@ def tile_morphable_face_decode_s10_kernel(tc, code, id_words, id_scales, ex_word
             bank_of[(kind, c, m)] = bank
 
         def ident_exit(c, m, eng):
-            t = work.tile([P, W], F32, name="im", bufs=14)
+            t = work.tile([P, W], F32, name="im", bufs=17)
             mu = mean[:, W * c : W * (c + 1)]
             bank = bank_of[("id", c, m)]
             if eng == "V":
@@ -280,231 +282,231 @@ def tile_morphable_face_decode_s10_kernel(tc, code, id_words, id_scales, ex_word
 
         code_transpose(0)
         mean_column()
-        code_copy(0)
+        code_copy(0, "S")
         mean_column_copy()
         code_codes(0)
         code_transpose(1)
         mean_spread(0, 2 * W)
-        code_copy(1)
-        mean_copy(0)
-        code_transpose(2)
-        code_codes(1)
-        code_transpose(3)
-        code_copy(2)
+        code_copy(1, "S")
         product("id", 0, 0)
-        code_copy(3)
-        code_codes(2)
-        interleave("S", 0, 0, 0, 256)
-        code_codes(3)
+        mean_copy(0)
+        code_codes(1)
+        code_transpose(2)
+        ident_exit(0, 0, "S")
+        code_transpose(3)
+        code_copy(2, "S")
+        ident_mean(0, 0)
         product("id", 0, 1)
-        ident_exit(0, 0, "V")
-        interleave("V", 0, 0, 256, 512)
+        code_copy(3, "S")
+        interleave("S", 0, 0, 0, 256)
+        code_codes(2)
+        code_codes(3)
         product("id", 0, 2)
-        interleave("S", 0, 1, 0, 256)
         ident_exit(0, 1, "V")
-        quantise(0, 0)
         product("id", 0, 3)
-        interleave("S", 0, 1, 256, 512)
+        interleave("S", 0, 0, 256, 512)
         ident_exit(0, 2, "V")
         mean_spread(2 * W, 4 * W)
-        ident_exit(0, 3, "V")
+        interleave("V", 0, 1, 0, 256)
         product("id", 1, 0)
+        interleave("S", 0, 1, 256, 512)
+        quantise(0, 0)
+        product("id", 1, 1)
+        ident_exit(0, 3, "V")
+        product("id", 1, 2)
         mean_copy(1)
-        quantise(0, 1)
         ident_exit(1, 0, "V")
+        product("id", 1, 3)
+        quantise(0, 1)
+        mean_spread(4 * W, 6 * W)
+        ident_exit(1, 3, "S")
+        ident_exit(1, 1, "V")
+        interleave("S", 1, 0, 0, 256)
+        ident_mean(1, 3)
+        product("id", 2, 0)
+        ident_exit(1, 2, "V")
+        product("id", 2, 1)
+        ident_exit(2, 0, "V")
+        product("id", 2, 2)
+        mean_copy(2)
+        ident_exit(2, 1, "V")
+        product("id", 2, 3)
+        interleave("S", 1, 0, 256, 512)
+        ident_exit(2, 2, "V")
         product("act", 0, 0)
+        ident_exit(2, 3, "V")
         product("ex", 0, 0)
         tanh(0, 0)
-        product("act", 0, 1)
-        interleave("S", 1, 0, 0, 256)
-        mul(0, 0)
-        product("ex", 0, 1)
-        interleave("V", 1, 0, 256, 512)
-        product("id", 1, 1)
-        tanh(0, 1)
-        interleave("V", 1, 1, 0, 256)
-        product("act", 0, 2)
-        interleave("S", 1, 1, 256, 512)
         quantise(1, 0)
-        product("ex", 0, 2)
-        mul(0, 1)
-        finish(0, 0, "G")
-        product("id", 1, 2)
-        tanh(0, 2)
-        ident_exit(1, 1, "V")
-        product("act", 0, 3)
-        product("ex", 0, 3)
-        interleave("S", 2, 0, 0, 256)
-        mul(0, 2)
-        finish(0, 1, "G")
-        product("id", 1, 3)
-        ident_exit(1, 2, "V")
-        mean_spread(4 * W, 6 * W)
-        finish(0, 2, "G")
-        load_exw(2)
-        ident_exit(1, 3, "V")
-        tanh(0, 3)
-        interleave("S", 2, 0, 256, 512)
-        product("id", 2, 0)
-        mul(0, 3)
-        product("id", 2, 1)
-        quantise(1, 1)
-        mean_copy(2)
-        ident_exit(2, 0, "V")
-        finish(0, 3, "G")
-        load_exw(3)
-        product("act", 1, 0)
-        interleave("S", 2, 1, 0, 256)
-        ident_exit(2, 1, "V")
-        product("ex", 1, 0)
-        product("act", 1, 1)
-        quantise(2, 0)
-        product("ex", 1, 1)
-        tanh(1, 0)
-        interleave("V", 2, 1, 256, 512)
-        product("act", 1, 2)
-        tanh(1, 1)
-        mul(1, 0)
-        product("ex", 1, 2)
-        tanh(1, 2)
-        quantise(2, 1)
-        product("id", 2, 2)
-        mul(1, 1)
-        finish(1, 0, "G")
-        load_act(4, 0, 2 * W)
-        product("act", 1, 3)
-        mul(1, 2)
-        product("ex", 1, 3)
-        interleave("S", 3, 0, 0, 256)
-        ident_exit(2, 2, "V")
-        finish(1, 1, "G")
-        load_act(4, 1, 2 * W)
-        product("id", 2, 3)
-        product("act", 2, 0)
-        ident_exit(2, 3, "V")
-        tanh(1, 3)
-        finish(1, 2, "G")
-        load_exw(4)
-        product("ex", 2, 0)
-        tanh(2, 0)
-        mul(1, 3)
         product("id", 3, 0)
-        interleave("S", 3, 0, 256, 512)
-        mul(2, 0)
-        finish(1, 3, "G")
-        load_exw(5)
-        product("act", 2, 1)
+        interleave("S", 1, 1, 0, 256)
+        mul(0, 0)
+        product("act", 0, 1)
         ident_exit(3, 0, "V")
+        product("ex", 0, 1)
+        tanh(0, 1)
+        finish(0, 0, "V")
+        load_act(4, 0, 2 * W)
+        product("id", 3, 1)
+        interleave("S", 1, 1, 256, 512)
+        mul(0, 1)
+        product("act", 0, 2)
+        ident_exit(3, 1, "V")
+        product("ex", 0, 2)
+        tanh(0, 2)
+        finish(0, 1, "V")
+        load_act(4, 1, 2 * W)
+        product("id", 3, 2)
+        interleave("S", 2, 0, 0, 256)
+        quantise(1, 1)
+        product("act", 0, 3)
+        mul(0, 2)
+        product("ex", 0, 3)
+        product("act", 1, 0)
+        ident_exit(3, 2, "V")
+        tanh(0, 3)
+        product("ex", 1, 0)
+        finish(0, 2, "V")
+        load_exw(4)
+        tanh(1, 0)
+        product("id", 3, 3)
+        mul(0, 3)
+        interleave("S", 2, 0, 256, 512)
+        product("act", 1, 1)
+        mul(1, 0)
+        product("ex", 1, 1)
+        finish(0, 3, "V")
+        load_exw(5)
+        tanh(1, 1)
+        product("id", 4, 0)
+        quantise(2, 0)
+        interleave("S", 2, 1, 0, 256)
+        product("act", 1, 2)
+        mul(1, 1)
+        product("ex", 1, 2)
+        finish(1, 0, "V")
+        tanh(1, 2)
+        product("act", 1, 3)
+        finish(1, 1, "V")
+        interleave("S", 2, 1, 256, 512)
+        product("ex", 1, 3)
+        mul(1, 2)
+        ident_exit(3, 3, "V")
+        tanh(1, 3)
+        quantise(2, 1)
+        product("id", 4, 1)
+        interleave("S", 3, 0, 0, 256)
+        mul(1, 3)
+        product("id", 4, 2)
+        finish(1, 2, "V")
+        product("act", 2, 0)
+        interleave("S", 3, 0, 256, 512)
+        finish(1, 3, "V")
+        ident_exit(4, 0, "V")
+        tanh(2, 0)
+        quantise(3, 0)
+        product("ex", 2, 0)
+        interleave("S", 3, 1, 0, 256)
+        ident_exit(4, 1, "V")
+        product("act", 2, 1)
+        mul(2, 0)
         product("ex", 2, 1)
         tanh(2, 1)
-        finish(2, 0, "G")
-        product("id", 3, 1)
-        interleave("S", 3, 1, 0, 256)
-        mul(2, 1)
-        product("act", 2, 2)
-        ident_exit(3, 1, "V")
-        finish(2, 1, "G")
-        product("ex", 2, 2)
-        tanh(2, 2)
-        product("id", 3, 2)
-        interleave("S", 3, 1, 256, 512)
-        mul(2, 2)
-        product("act", 2, 3)
-        product("ex", 2, 3)
-        quantise(3, 0)
-        product("id", 3, 3)
-        tanh(2, 3)
-        ident_exit(3, 2, "V")
-        finish(2, 2, "G")
-        product("id", 4, 0)
-        interleave("S", 4, 0, 0, 256)
-        ident_exit(3, 3, "V")
-        product("id", 4, 1)
-        mul(2, 3)
-        product("id", 4, 2)
-        quantise(3, 1)
-        interleave("S", 4, 0, 256, 512)
-        ident_exit(4, 0, "V")
-        finish(2, 3, "G")
-        product("act", 3, 0)
-        ident_exit(4, 1, "V")
-        product("ex", 3, 0)
-        tanh(3, 0)
         ident_exit(4, 2, "V")
-        product("act", 3, 1)
-        interleave("S", 4, 1, 0, 256)
-        mul(3, 0)
-        product("ex", 3, 1)
-        quantise(4, 0)
-        product("act", 3, 2)
-        tanh(3, 1)
-        product("ex", 3, 2)
-        interleave("V", 4, 1, 256, 512)
-        tanh(3, 2)
-        product("act", 3, 3)
-        mul(3, 1)
-        finish(3, 0, "G")
-        product("ex", 3, 3)
-        interleave("S", 5, 0, 0, 256)
-        mul(3, 2)
+        product("act", 2, 2)
+        interleave("S", 3, 1, 256, 512)
+        product("ex", 2, 2)
+        mul(2, 1)
         product("id", 4, 3)
-        finish(3, 1, "G")
+        finish(2, 0, "V")
+        product("act", 2, 3)
+        tanh(2, 2)
+        finish(2, 1, "V")
+        product("ex", 2, 3)
+        quantise(3, 1)
+        tanh(2, 3)
         product("id", 5, 0)
-        ident_exit(4, 3, "V")
-        tanh(3, 3)
+        interleave("S", 4, 0, 0, 256)
+        mul(2, 2)
+        product("act", 3, 0)
+        mul(2, 3)
+        product("ex", 3, 0)
+        finish(2, 2, "V")
+        tanh(3, 0)
         product("id", 5, 1)
+        finish(2, 3, "V")
+        interleave("S", 4, 0, 256, 512)
+        product("act", 3, 1)
+        mul(3, 0)
+        ident_exit(4, 3, "V")
+        tanh(3, 1)
+        quantise(4, 0)
+        product("ex", 3, 1)
+        interleave("S", 4, 1, 0, 256)
+        finish(3, 0, "V")
+        product("act", 3, 2)
+        mul(3, 1)
+        product("ex", 3, 2)
+        tanh(3, 2)
         ident_exit(5, 0, "V")
-        interleave("S", 5, 0, 256, 512)
-        finish(3, 2, "G")
+        interleave("S", 4, 1, 256, 512)
+        mul(3, 2)
         product("id", 5, 2)
+        finish(3, 1, "V")
+        product("act", 3, 3)
+        interleave("S", 5, 0, 0, 256)
+        quantise(4, 1)
+        product("ex", 3, 3)
+        finish(3, 2, "V")
+        tanh(3, 3)
+        ident_exit(5, 1, "V")
+        interleave("S", 5, 0, 256, 512)
         mul(3, 3)
         product("id", 5, 3)
-        ident_exit(5, 1, "V")
-        interleave("S", 5, 1, 0, 256)
-        finish(3, 3, "G")
         ident_exit(5, 2, "V")
-        ident_exit(5, 3, "V")
-        interleave("S", 5, 1, 256, 512)
-        quantise(4, 1)
-        quantise(5, 0)
         product("act", 4, 0)
-        quantise(5, 1)
+        interleave("S", 5, 1, 0, 256)
+        quantise(5, 0)
         product("ex", 4, 0)
-        tanh(4, 0)
+        finish(3, 3, "V")
         product("act", 4, 1)
-        mul(4, 0)
+        tanh(4, 0)
         product("ex", 4, 1)
+        ident_exit(5, 3, "V")
         tanh(4, 1)
-        finish(4, 0, "G")
         product("act", 4, 2)
-        mul(4, 1)
+        mul(4, 0)
+        interleave("S", 5, 1, 256, 512)
         product("ex", 4, 2)
-        tanh(4, 2)
-        finish(4, 1, "G")
+        mul(4, 1)
         product("act", 4, 3)
-        mul(4, 2)
+        finish(4, 0, "V")
         product("ex", 4, 3)
+        tanh(4, 2)
+        finish(4, 1, "V")
         tanh(4, 3)
-        finish(4, 2, "G")
+        quantise(5, 1)
+        mul(4, 2)
         product("act", 5, 0)
         mul(4, 3)
         product("ex", 5, 0)
         tanh(5, 0)
-        finish(4, 3, "G")
+        finish(4, 2, "V")
         product("act", 5, 1)
-        mul(5, 0)
+        finish(4, 3, "V")
         product("ex", 5, 1)
         tanh(5, 1)
-        finish(5, 0, "G")
         product("act", 5, 2)
-        mul(5, 1)
+        mul(5, 0)
         product("ex", 5, 2)
+        mul(5, 1)
         tanh(5, 2)
         product("act", 5, 3)
-        finish(5, 1, "G")
-        mul(5, 2)
+        finish(5, 0, "V")
         product("ex", 5, 3)
+        finish(5, 1, "V")
         tanh(5, 3)
-        finish(5, 2, "V")
+        mul(5, 2)
         mul(5, 3)
+        finish(5, 2, "V")
         finish(5, 3, "V")

from contextlib import ExitStack

import concourse.mybir as mybir
from concourse.masks import make_identity

M, K, N = 512, 1024, 3072
FLOPS = 3 * 2 * M * K * N

F32 = mybir.dt.float32
BF16 = mybir.dt.bfloat16
I32 = mybir.dt.int32
U32 = mybir.dt.uint32
U8 = mybir.dt.uint8
FP8X4 = mybir.dt.float8_e4m3fn_x4
FP4X4 = mybir.dt.float4_e2m1fn_x4
ACT = mybir.ActivationFunctionType
ALU = mybir.AluOpType

P = 128
G = K // 512
W = 512
CHUNKS = N // W
MT = M // P


def tile_morphable_face_decode_s10_kernel(tc, code, id_words, id_scales, ex_words, ex_scales, act_basis, mean_shape, out):
    nc = tc.nc
    with ExitStack() as ctx:
        keep = ctx.enter_context(tc.tile_pool(name="keep", bufs=1))
        work = ctx.enter_context(tc.tile_pool(name="work", bufs=3))
        psum = ctx.enter_context(tc.psum_pool(name="psum", bufs=8))
        ctx.enter_context(tc.manual_schedule())

        mrow = keep.tile([P, P], BF16, name="mrow", align_bytes=64)
        nc.vector.memset(mrow[:].bitcast(I32), 0)
        nc.gpsimd.dma_start(out=mrow[0 : N // P, :], in_=mean_shape.rearrange("(c p) -> c p", p=P))
        ident = keep.tile([P, P], F32, name="ident")
        make_identity(nc, ident[:])
        idw = {}
        exw = {}
        raw = {}
        idp = {}
        craw = []

        def load_code(m0, count):
            t = keep.tile([P, count, K], BF16, name="craw%d" % m0, align_bytes=64)
            nc.sync.dma_start(out=t[:], in_=code[m0 * P : (m0 + count) * P, :].rearrange("(m p) k -> p m k", p=P))
            craw.extend((t, i) for i in range(count))

        def load_idw(c, width):
            t = keep.tile([P, G, 2 * width], U8, name="idw%d" % c, align_bytes=64)
            nc.sync.dma_start(
                out=t[:].bitcast(I32),
                in_=id_words[:, :, 2 * W * c : 2 * W * c + 2 * width].rearrange("g p b -> p g b").bitcast(I32),
            )
            for i in range(width // W):
                idw[c + i] = (t, 2 * W * i)

        def make_idp(c, count, eng):
            t = keep.tile([P, G, count * W], U8, name="idp%d" % c, align_bytes=64)
            eng.memset(t[:].rearrange("p g n -> p (g n)").bitcast(I32), 0)
            for i in range(count):
                idp[c + i] = (t, W * i)

        def load_idp(c, count, eng):
            t = idp[c][0]
            for q in range(4):
                eng.dma_start(
                    out=t[32 * q : 32 * q + 4, :, :].bitcast(I32),
                    in_=id_scales[:, 4 * q : 4 * q + 4, W * c : W * (c + count)].rearrange("g r n -> r g n").bitcast(I32),
                )

        make_idp(0, 2, nc.vector)
        load_code(0, 1)
        load_idw(0, W)
        load_idp(0, 2, nc.scalar)
        load_code(1, 1)
        load_code(2, 2)
        warm = keep.tile([P, 1], F32, name="warm")
        nc.scalar.activation(out=warm[:], in_=ident[:, 0:1], func=ACT.Tanh)
        identb = keep.tile([P, P], BF16, name="identb")
        nc.vector.tensor_copy(out=identb[:], in_=ident[:])
        make_idp(2, 4, nc.gpsimd)
        exp = keep.tile([P, N], U8, name="exp", align_bytes=64)
        nc.gpsimd.memset(exp[:].bitcast(I32), 0)
        mean = keep.tile([P, N], BF16, name="mean", align_bytes=64)
        def load_exw(c):
            t = keep.tile([P, G, 4 * W], U8, name="exw%d" % c, align_bytes=64)
            nc.sync.dma_start(
                out=t[:].bitcast(I32),
                in_=ex_words.rearrange("g p n t -> p g (n t)")[:, :, 4 * W * c : 4 * W * (c + 1)].bitcast(I32),
            )
            exw[c] = t

        def load_act(c, g, width):
            t = keep.tile([P, 4, width], BF16, name="raw%d_%d" % (c, g), align_bytes=64)
            nc.sync.dma_start(
                out=t[:],
                in_=act_basis[512 * g : 512 * (g + 1), W * c : W * c + width].rearrange("(p t) n -> p t n", t=4),
            )
            for i in range(width // W):
                raw[(c + i, g)] = (t, W * i)

        def load_mean(a):
            nc.sync.dma_start(out=mean[:, a:N], in_=mean_shape[a:N].partition_broadcast(P))

        def load_exs():
            for q in range(4):
                nc.sync.dma_start(
                    out=exp[32 * q + 4 : 32 * q + 12, :].bitcast(I32),
                    in_=ex_scales[:, 4 * q : 4 * q + 4, :].bitcast(I32),
                )

        load_idw(1, W)
        load_act(0, 0, W)
        load_act(0, 1, W)
        load_idp(2, 4, nc.sync)
        load_idw(2, 2 * W)
        load_exw(0)
        load_exs()
        load_act(1, 0, W)
        load_act(1, 1, W)
        load_act(2, 0, W)
        load_act(2, 1, W)
        load_exw(1)
        load_idw(4, 2 * W)
        load_act(3, 0, W)
        load_act(3, 1, W)
        load_exw(2)
        load_exw(3)

        def mean_spread(a, b):
            bank = psum.tile([P, b - a], BF16, name="bank")
            for j in range((b - a) // P):
                c = a // P + j
                nc.tensor.transpose(bank[:, P * j : P * (j + 1)], mcol[:, c : c + 1].to_broadcast([P, P]), identb[:])
            mbanks[a // (2 * W)] = bank

        def mean_copy(i):
            nc.scalar.copy(out=mean[:, 2 * W * i : 2 * W * (i + 1)], in_=mbanks[i][:])

        ccode, cscale, cgrp, cbank = {}, {}, {}, {}

        def code_transpose(m):
            bank = psum.tile([P, G, 2, P], F32, name="bank")
            t, i = craw[m]
            words = t[:, i, :].bitcast(F32)
            for g in range(G):
                for u in range(2):
                    nc.tensor.transpose(bank[:, g, u, :], words[:, 256 * g + u : 256 * (g + 1) : 2], ident[:])
            cbank[m] = bank

        def code_copy(m, eng):
            t = keep.tile([P, G, P, 4], BF16, name="cgrp%d" % m, align_bytes=64)
            dst = t[:].rearrange("p g m t -> p (g m t)").bitcast(F32).rearrange("p (g m u) -> p g m u", g=G, u=2)
            src = cbank[m][:].rearrange("p g u m -> p g m u")
            if eng == "S":
                nc.scalar.copy(out=dst, in_=src)
            else:
                nc.vector.tensor_copy(out=dst, in_=src)
            cgrp[m] = t

        def code_codes(m):
            t = cgrp[m]
            cc = keep.tile([P, G, P], U32, name="ccode%d" % m, align_bytes=64)
            cs = keep.tile([P, G, P], U8, name="cscale%d" % m, align_bytes=64)
            nc.vector.quantize_mx(
                out=cc[:].rearrange("p g m -> p (g m)").bitcast(FP8X4),
                scales=cs[:].rearrange("p g m -> p (g m)"),
                in_=t[:].rearrange("p g m t -> p (g m t)"),
            )
            ccode[m] = cc
            cscale[m] = cs

        mcol = keep.tile([P, CHUNKS * MT], BF16, name="mcol")
        mbanks = {}

        def mean_column():
            mbanks["col"] = psum.tile([P, P], BF16, name="bank")
            nc.tensor.transpose(mbanks["col"][:], mrow[:], identb[:])

        def mean_column_copy():
            nc.vector.tensor_copy(out=mcol[:], in_=mbanks["col"][:, 0 : CHUNKS * MT])


        grp = {}
        acode, ascale = {}, {}
        im = {}
        bank_of = {}

        def interleave(eng, c, g, a, b):
            if (c, g) not in grp:
                grp[(c, g)] = work.tile([P, W, 4], BF16, name="grp%d" % g, align_bytes=64)
            t, off = raw[(c, g)]
            src = t[:, :, off + a : off + b].rearrange("p t (c i) -> p c t i", i=4)
            dst = grp[(c, g)][:, a:b, :].rearrange("p (c i) t -> p c t i", i=4)
            if eng == "S":
                nc.scalar.copy(out=dst, in_=src)
            elif eng == "V":
                nc.vector.tensor_copy(out=dst, in_=src)
            else:
                nc.gpsimd.tensor_scalar(out=dst, in0=src, scalar1=1.0, scalar2=0.0, op0=ALU.mult, op1=ALU.add)

        def quantise(c, g):
            cc = keep.tile([P, W], U32, name="acode%d_%d" % (c, g), align_bytes=64)
            cs = keep.tile([P, W], U8, name="ascale%d_%d" % (c, g), align_bytes=64)
            nc.vector.quantize_mx(out=cc[:].bitcast(FP8X4), scales=cs[:], in_=grp[(c, g)][:].rearrange("p n t -> p (n t)"))
            acode[(c, g)] = cc
            ascale[(c, g)] = cs

        def product(kind, c, m):
            bank = psum.tile([P, W], F32, name="bank")
            for g in range(G):
                if kind == "id":
                    t, off = idw[c]
                    rhs = t[:, g, off : off + 2 * W].bitcast(FP4X4)
                    sp, so = idp[c]
                    rhs_scale = sp[:, g, so : so + W]
                elif kind == "ex":
                    rhs = exw[c][:, g, :].bitcast(FP8X4)
                    rhs_scale = exp[4 + 4 * g : P, W * c : W * (c + 1)]
                else:
                    rhs = acode[(c, g)][:].bitcast(FP8X4)
                    rhs_scale = ascale[(c, g)][:]
                nc.tensor.matmul_mx(
                    out=bank[:],
                    lhsT=ccode[m][:, g, :].bitcast(FP8X4),
                    lhsT_scale=cscale[m][:, g, :],
                    rhs=rhs,
                    rhs_scale=rhs_scale,
                    start=(g == 0),
                    stop=(g == G - 1),
                )
            bank_of[(kind, c, m)] = bank

        def ident_exit(c, m, eng):
            t = work.tile([P, W], F32, name="im", bufs=17)
            mu = mean[:, W * c : W * (c + 1)]
            bank = bank_of[("id", c, m)]
            if eng == "V":
                nc.vector.tensor_tensor(out=t[:], in0=bank[:], in1=mu, op=ALU.add)
            else:
                nc.scalar.copy(out=t[:], in_=bank[:])
            im[(c, m)] = t

        def ident_mean(c, m):
            t = im[(c, m)]
            nc.gpsimd.tensor_tensor(out=t[:], in0=t[:], in1=mean[:, W * c : W * (c + 1)], op=ALU.add)

        th = {}

        def tanh(c, m):
            t = work.tile([P, W], F32, name="th")
            nc.scalar.activation(out=t[:], in_=bank_of[("act", c, m)][:], func=ACT.Tanh)
            th[(c, m)] = t

        ob = {}

        def last_tile(c, m, parts):
            mu = mean[:, W * c : W * (c + 1)]
            t = work.tile([P, W], F32, name="ob", bufs=9)
            nc.vector.tensor_tensor(out=t[:], in0=bank_of[("ex", c, m)][:], in1=th[(c, m)][:], op=ALU.mult)
            nc.vector.tensor_tensor(out=t[:], in0=t[:], in1=mu, op=ALU.add)
            product("id", c, m)
            bank = bank_of[("id", c, m)]
            for i in range(parts):
                cols = slice(W // parts * i, W // parts * (i + 1))
                o = work.tile([P, W // parts], F32, name="lob", bufs=2)
                nc.vector.tensor_tensor(out=o[:], in0=bank[:, cols], in1=t[:, cols], op=ALU.add)
                nc.sync.dma_start(out=out[m * P : (m + 1) * P, W * c + cols.start : W * c + cols.stop], in_=o[:])

        def mul(c, m):
            t = work.tile([P, W], F32, name="ob", bufs=9)
            nc.vector.tensor_tensor(out=t[:], in0=bank_of[("ex", c, m)][:], in1=th[(c, m)][:], op=ALU.mult)
            ob[(c, m)] = t

        def finish(c, m, eng):
            t = ob[(c, m)]
            e = nc.vector if eng == "V" else nc.gpsimd
            e.tensor_tensor(out=t[:], in0=t[:], in1=im[(c, m)][:], op=ALU.add)
            nc.sync.dma_start(out=out[m * P : (m + 1) * P, W * c : W * (c + 1)], in_=t[:])

        code_transpose(0)
        mean_column()
        code_copy(0, "S")
        mean_column_copy()
        code_codes(0)
        code_transpose(1)
        mean_spread(0, 2 * W)
        code_copy(1, "S")
        product("id", 0, 0)
        mean_copy(0)
        code_codes(1)
        code_transpose(2)
        ident_exit(0, 0, "S")
        code_transpose(3)
        code_copy(2, "S")
        ident_mean(0, 0)
        product("id", 0, 1)
        code_copy(3, "S")
        interleave("S", 0, 0, 0, 256)
        code_codes(2)
        code_codes(3)
        product("id", 0, 2)
        ident_exit(0, 1, "V")
        product("id", 0, 3)
        interleave("S", 0, 0, 256, 512)
        ident_exit(0, 2, "V")
        mean_spread(2 * W, 4 * W)
        interleave("V", 0, 1, 0, 256)
        product("id", 1, 0)
        interleave("S", 0, 1, 256, 512)
        quantise(0, 0)
        product("id", 1, 1)
        ident_exit(0, 3, "V")
        product("id", 1, 2)
        mean_copy(1)
        ident_exit(1, 0, "V")
        product("id", 1, 3)
        quantise(0, 1)
        mean_spread(4 * W, 6 * W)
        ident_exit(1, 3, "S")
        ident_exit(1, 1, "V")
        interleave("S", 1, 0, 0, 256)
        ident_mean(1, 3)
        product("id", 2, 0)
        ident_exit(1, 2, "V")
        product("id", 2, 1)
        ident_exit(2, 0, "V")
        product("id", 2, 2)
        mean_copy(2)
        ident_exit(2, 1, "V")
        product("id", 2, 3)
        interleave("S", 1, 0, 256, 512)
        ident_exit(2, 2, "V")
        product("act", 0, 0)
        ident_exit(2, 3, "V")
        product("ex", 0, 0)
        tanh(0, 0)
        quantise(1, 0)
        product("id", 3, 0)
        interleave("S", 1, 1, 0, 256)
        mul(0, 0)
        product("act", 0, 1)
        ident_exit(3, 0, "V")
        product("ex", 0, 1)
        tanh(0, 1)
        finish(0, 0, "V")
        load_act(4, 0, 2 * W)
        product("id", 3, 1)
        interleave("S", 1, 1, 256, 512)
        mul(0, 1)
        product("act", 0, 2)
        ident_exit(3, 1, "V")
        product("ex", 0, 2)
        tanh(0, 2)
        finish(0, 1, "V")
        load_act(4, 1, 2 * W)
        product("id", 3, 2)
        interleave("S", 2, 0, 0, 256)
        quantise(1, 1)
        product("act", 0, 3)
        mul(0, 2)
        product("ex", 0, 3)
        product("act", 1, 0)
        ident_exit(3, 2, "V")
        tanh(0, 3)
        product("ex", 1, 0)
        finish(0, 2, "V")
        load_exw(4)
        tanh(1, 0)
        product("id", 3, 3)
        mul(0, 3)
        interleave("S", 2, 0, 256, 512)
        product("act", 1, 1)
        mul(1, 0)
        product("ex", 1, 1)
        finish(0, 3, "V")
        load_exw(5)
        tanh(1, 1)
        product("id", 4, 0)
        quantise(2, 0)
        interleave("S", 2, 1, 0, 256)
        product("act", 1, 2)
        mul(1, 1)
        product("ex", 1, 2)
        finish(1, 0, "V")
        tanh(1, 2)
        product("act", 1, 3)
        finish(1, 1, "V")
        interleave("S", 2, 1, 256, 512)
        product("ex", 1, 3)
        mul(1, 2)
        ident_exit(3, 3, "V")
        tanh(1, 3)
        quantise(2, 1)
        product("id", 4, 1)
        interleave("S", 3, 0, 0, 256)
        mul(1, 3)
        product("id", 4, 2)
        finish(1, 2, "V")
        product("act", 2, 0)
        interleave("S", 3, 0, 256, 512)
        finish(1, 3, "V")
        ident_exit(4, 0, "V")
        tanh(2, 0)
        quantise(3, 0)
        product("ex", 2, 0)
        interleave("S", 3, 1, 0, 256)
        ident_exit(4, 1, "V")
        product("act", 2, 1)
        mul(2, 0)
        product("ex", 2, 1)
        tanh(2, 1)
        ident_exit(4, 2, "V")
        product("act", 2, 2)
        interleave("S", 3, 1, 256, 512)
        product("ex", 2, 2)
        mul(2, 1)
        product("id", 4, 3)
        finish(2, 0, "V")
        product("act", 2, 3)
        tanh(2, 2)
        finish(2, 1, "V")
        product("ex", 2, 3)
        quantise(3, 1)
        tanh(2, 3)
        product("id", 5, 0)
        interleave("S", 4, 0, 0, 256)
        mul(2, 2)
        product("act", 3, 0)
        mul(2, 3)
        product("ex", 3, 0)
        finish(2, 2, "V")
        tanh(3, 0)
        product("id", 5, 1)
        finish(2, 3, "V")
        interleave("S", 4, 0, 256, 512)
        product("act", 3, 1)
        mul(3, 0)
        ident_exit(4, 3, "V")
        tanh(3, 1)
        quantise(4, 0)
        product("ex", 3, 1)
        interleave("S", 4, 1, 0, 256)
        finish(3, 0, "V")
        product("act", 3, 2)
        mul(3, 1)
        product("ex", 3, 2)
        tanh(3, 2)
        ident_exit(5, 0, "V")
        interleave("S", 4, 1, 256, 512)
        mul(3, 2)
        product("id", 5, 2)
        finish(3, 1, "V")
        product("act", 3, 3)
        interleave("S", 5, 0, 0, 256)
        quantise(4, 1)
        product("ex", 3, 3)
        finish(3, 2, "V")
        tanh(3, 3)
        ident_exit(5, 1, "V")
        interleave("S", 5, 0, 256, 512)
        mul(3, 3)
        product("id", 5, 3)
        ident_exit(5, 2, "V")
        product("act", 4, 0)
        interleave("S", 5, 1, 0, 256)
        quantise(5, 0)
        product("ex", 4, 0)
        finish(3, 3, "V")
        product("act", 4, 1)
        tanh(4, 0)
        product("ex", 4, 1)
        ident_exit(5, 3, "V")
        tanh(4, 1)
        product("act", 4, 2)
        mul(4, 0)
        interleave("S", 5, 1, 256, 512)
        product("ex", 4, 2)
        mul(4, 1)
        product("act", 4, 3)
        finish(4, 0, "V")
        product("ex", 4, 3)
        tanh(4, 2)
        finish(4, 1, "V")
        tanh(4, 3)
        quantise(5, 1)
        mul(4, 2)
        product("act", 5, 0)
        mul(4, 3)
        product("ex", 5, 0)
        tanh(5, 0)
        finish(4, 2, "V")
        product("act", 5, 1)
        finish(4, 3, "V")
        product("ex", 5, 1)
        tanh(5, 1)
        product("act", 5, 2)
        mul(5, 0)
        product("ex", 5, 2)
        mul(5, 1)
        tanh(5, 2)
        product("act", 5, 3)
        finish(5, 0, "V")
        product("ex", 5, 3)
        finish(5, 1, "V")
        tanh(5, 3)
        mul(5, 2)
        mul(5, 3)
        finish(5, 2, "V")
        finish(5, 3, "V")
